import numpy as np
import ml_dtypes


def mxq(x, axis, fmt="e4m3"):
    dtype, down = {"e4m3": (ml_dtypes.float8_e4m3fn, 7), "e5m2": (ml_dtypes.float8_e5m2, 14)}[fmt]
    v = np.moveaxis(np.asarray(x, np.float32).astype(ml_dtypes.bfloat16).astype(np.float64), axis, -1)
    blocks = v.reshape(v.shape[:-1] + (-1, 32))
    amax = np.abs(blocks).max(-1, keepdims=True)
    byte = np.maximum(np.where(amax > 0, np.frexp(amax)[1] - 1 + 127, 0) - down, 1)
    scale = np.exp2(byte - 127.0)
    codes = (blocks / scale).astype(np.float32).astype(dtype).astype(np.float64)
    return np.moveaxis((codes * scale).reshape(v.shape), -1, axis)


WIDE = False


def mx_kscale(k):
    if not WIDE:
        return np.ones(k)
    levels = np.array([10, -10, 5, -5, 0])
    if k % 512:
        return np.exp2(np.random.permutation(np.resize(levels, k // 32))).repeat(32)
    a = np.empty((k // 512, 16))
    for p in range(k // 512):
        a[p, :8] = np.random.permutation(np.resize(levels, 8))
        for g in range(8):
            far = levels[np.abs(levels - a[p, g]) >= 10]
            a[p, g + 8] = far[np.random.randint(len(far))]
    return np.exp2(a.ravel()).repeat(32)


BF16 = ml_dtypes.bfloat16


def bf(x):
    return np.asarray(x, np.float32).astype(BF16)


def f64(x):
    return np.asarray(x).astype(np.float64)


E2M1 = np.array([0.0, 0.5, 1.0, 1.5, 2.0, 3.0, 4.0, 6.0, -0.0, -0.5, -1.0, -1.5, -2.0, -3.0, -4.0, -6.0])


def pack_weight(w, fmt):
    k, n = w.shape
    w = f64(bf(w)).reshape(k // 32, 32, n)
    amax = np.abs(w).max(1)
    if fmt == "e4m3":
        byte = np.frexp(amax)[1] - 1 + 127 - 7
    else:
        mant, ex = np.frexp(amax / 6.0)
        byte = np.where(mant > 0.5, ex, ex - 1) + 127
    byte = np.clip(np.where(amax > 0, byte, 1), 1, 254)
    scaled = (w * np.exp2(127.0 - byte)[:, None, :]).reshape(k, n).astype(np.float32)
    by_word = np.ascontiguousarray(scaled.reshape(k // 512, 128, 4, n).transpose(0, 1, 3, 2))
    if fmt == "e4m3":
        words = by_word.astype(ml_dtypes.float8_e4m3fn).view(np.uint8)
    else:
        c = by_word.astype(ml_dtypes.float4_e2m1fn).view(np.uint8) & 0xF
        words = c[..., 0::2] | (c[..., 1::2] << 4)
    return np.ascontiguousarray(words), np.ascontiguousarray(byte.astype(np.uint8).reshape(k // 512, 16, n))


def unpack_weight(words, scales, fmt):
    g, p, n, _ = words.shape
    if fmt == "e4m3":
        vals = np.ascontiguousarray(words).view(ml_dtypes.float8_e4m3fn).astype(np.float64)
    else:
        nib = np.empty((g, p, n, 4), np.uint8)
        nib[..., 0::2] = words & 0xF
        nib[..., 1::2] = words >> 4
        vals = E2M1[nib]
    vals = vals * np.repeat(np.exp2(scales.astype(np.float64) - 127.0), 8, axis=1)[..., None]
    return vals.transpose(0, 1, 3, 2).reshape(g * 512, n)
def pack4(w):
    words, scales = pack_weight(w, "e2m1")
    return words.reshape(words.shape[0], 128, -1), scales


def unpack4(words, scales):
    return unpack_weight(words.reshape(words.shape[0], 128, -1, 2), scales, "e2m1")


E4M3FN = np.array([(-1.0 if i & 128 else 1.0) * ((1.0 + (i & 7) / 8.0) * 2.0 ** (((i >> 3) & 15) - 7) if i & 120 else (i & 7) * 2.0 ** -9) for i in range(256)])


def e4m3fn_bytes(y):
    return np.clip(np.asarray(y, np.float64), -448.0, 448.0).astype(np.float32).astype(ml_dtypes.float8_e4m3fn).view(np.uint8)


def e4m3fn_values(b):
    return E4M3FN[b]


T, K, N, B = 1024, 2048, 1024, 128


def setup_inputs():
    s = mx_kscale(K)
    t = mx_kscale(N)
    x = np.tanh(np.random.standard_normal((T, K))) * s
    x_scale = (np.abs(x).reshape(T, K // B, B).max(axis=2) / 448.0).astype(np.float32)
    x_bytes = e4m3fn_bytes(x / np.repeat(f64(x_scale), B, axis=1))
    w_fb_words, w_fb_scales = pack4(np.random.standard_normal((N, K)) / np.sqrt(N) / t[:, None])
    return {"x_bytes": x_bytes,
            "x_scale": x_scale,
            "w_out": bf(1.5 * np.random.standard_normal((N, K)) / np.sqrt(K) / s),
            "b_out": bf(0.5 * np.random.standard_normal(N)),
            "fb_gain": bf((1 + 0.1 * np.random.standard_normal(N)) * t),
            "w_fb_words": w_fb_words,
            "w_fb_scales": w_fb_scales,
            "drive": bf(0.5 * np.random.standard_normal((T, K)))}


def reference(x_bytes, x_scale, w_out, b_out, fb_gain, w_fb_words, w_fb_scales, drive):
    x = e4m3fn_values(x_bytes) * np.repeat(f64(x_scale), B, axis=1)
    y = (mxq(x, 1, "e4m3") @ mxq(f64(w_out), 1, "e4m3").T) + f64(b_out)
    z = y * f64(fb_gain)
    f = mxq(z, 1, "e4m3") @ unpack4(w_fb_words, w_fb_scales)
    state = np.tanh(f + f64(drive))
    return y, state

@@ -1,0 +1,330 @@
+from contextlib import ExitStack
+
+import concourse.mybir as mybir
+from concourse.masks import make_identity
+
+T, K, N = 1024, 2048, 1024
+FLOPS = 2 * T * K * N * 2
+
+F32 = mybir.dt.float32
+BF16 = mybir.dt.bfloat16
+I32 = mybir.dt.int32
+U32 = mybir.dt.uint32
+U8 = mybir.dt.uint8
+FP8 = mybir.dt.float8_e4m3fn
+FP8X4 = mybir.dt.float8_e4m3fn_x4
+FP4X4 = mybir.dt.float4_e2m1fn_x4
+ALU = mybir.AluOpType
+ACT = mybir.ActivationFunctionType
+
+P = 128
+TILES = T // P
+G1 = K // 512
+G2 = N // 512
+BLOCKS = K // 128
+QUARTERS = 4
+VECTOR_WIDENS = 5
+Z_ON_POOL = False
+
+
+def tile_reservoir_readout_feedback_d4_kernel(
+    tc, x_bytes, x_scale, w_out, b_out, fb_gain, w_fb_words, w_fb_scales, drive, out_0, out_1
+):
+    nc = tc.nc
+    with ExitStack() as ctx:
+        keep = ctx.enter_context(tc.tile_pool(name="keep", bufs=1))
+        work = ctx.enter_context(tc.tile_pool(name="work", bufs=2))
+        psum = ctx.enter_context(tc.psum_pool(name="psum", bufs=8))
+        ctx.enter_context(tc.manual_schedule(engines={mybir.EngineType.PE}))
+
+        def bank(k, shape, dtype, name):
+            return psum.tile(shape, dtype, name=name, tag="bank")
+
+        ident = keep.tile([P, P], F32, name="ident")
+        bias_words = keep.tile([P, 4], F32, name="bias_words")
+        gain_words = keep.tile([P, 4], F32, name="gain_words")
+        warm = keep.tile([P, 1], F32, name="warm")
+        fb_scale = keep.tile([P, G2, K], U8, name="fb_scale", align_bytes=64)
+        fb_words = keep.tile([P, G2, 2 * K], U8, name="fb_words", align_bytes=64)
+        bias = keep.tile([P, N], BF16, name="bias")
+        gain = keep.tile([P, N], BF16, name="gain")
+        w_codes = keep.tile([P, G1, N], U32, name="w_codes", align_bytes=64)
+        w_scale = keep.tile([P, G1, N], U8, name="w_scale", align_bytes=64)
+        xs = keep.tile([P, TILES, BLOCKS], F32, name="xs")
+
+        nc.vector.memset(warm[:], 0.0)
+        make_identity(nc, ident[:])
+        nc.gpsimd.memset(fb_scale[:].rearrange("p g n -> p (g n)").bitcast(I32), 0)
+        nc.scalar.activation(out=warm[:], in_=warm[:], func=ACT.Tanh)
+
+        x8 = [keep.tile([P, K], U8, name="xbytes%d" % i) for i in range(TILES)]
+        w_raw = [work.tile([P, K], BF16, name="w_raw%d" % r, tag="row4k", bufs=TILES) for r in range(TILES)]
+        drv = [keep.tile([P, K], BF16, name="drv%d" % i) for i in range(TILES)]
+
+        def load_x(i):
+            nc.sync.dma_start(out=x8[i][:], in_=x_bytes[i * P : (i + 1) * P, :])
+
+        def load_w(r):
+            nc.sync.dma_start(out=w_raw[r][:], in_=w_out[r * P : (r + 1) * P, :])
+
+        scale_rows = x_scale.rearrange("(i p) j -> p i j", p=P)
+        nc.sync.dma_start(out=xs[:, 0, :], in_=scale_rows[:, 0, :])
+        load_x(0)
+        nc.sync.dma_start(out=bias_words[:].bitcast(BF16), in_=b_out.rearrange("(p j) -> p j", p=P))
+        nc.sync.dma_start(out=gain_words[:].bitcast(BF16), in_=fb_gain.rearrange("(p j) -> p j", p=P))
+        load_w(0)
+        load_w(1)
+        nc.sync.dma_start(out=xs[:, 1:, :], in_=scale_rows[:, 1:, :])
+        load_x(1)
+        load_w(2)
+        load_w(3)
+        load_x(2)
+        for r in range(4, 8):
+            load_w(r)
+        load_x(3)
+        for q in range(4):
+            nc.sync.dma_start(
+                out=fb_scale[32 * q : 32 * q + 4, :, :].bitcast(I32),
+                in_=w_fb_scales[:, 4 * q : 4 * q + 4, :].rearrange("g r n -> r g n").bitcast(I32),
+            )
+        for g in range(G2):
+            nc.sync.dma_start(out=fb_words[:, g, :].bitcast(I32), in_=w_fb_words[g].bitcast(I32))
+        for i in range(TILES):
+            nc.sync.dma_start(out=drv[i][:], in_=drive[i * P : (i + 1) * P, :])
+            if 4 + i < TILES:
+                load_x(4 + i)
+
+        x_wide, x_turned, x_codes, x_scl = {}, {}, {}, {}
+        y_acc, y_sb, z_wide, z_turned, z_codes, z_scl, f_acc, state = {}, {}, {}, {}, {}, {}, {}, {}
+        turn_count = [0]
+
+        def turn_bank(nbanks, name):
+            turn_count[0] += 1
+            return bank(turn_count[0] % nbanks, [P, 4, P], F32, name)
+
+        def widen(i, blocks):
+            if i not in x_wide:
+                x_wide[i] = work.tile([P, K], BF16, name="x_wide%d" % i, tag="x_wide", bufs=4)
+            for j in blocks:
+                src = x8[i][:, j * 128 : (j + 1) * 128].bitcast(FP8)
+                if i < VECTOR_WIDENS:
+                    g, q = divmod(j, 4)
+                    dst = x_wide[i][:].rearrange("t (g u p e) -> t g p u e", g=G1, u=2, e=2)[:, g, 32 * q : 32 * q + 32]
+                    nc.vector.tensor_scalar(
+                        out=dst, in0=src.rearrange("t (p u e) -> t p u e", u=2, e=2),
+                        scalar1=xs[:, i, j : j + 1], scalar2=None, op0=ALU.mult,
+                    )
+                else:
+                    nc.scalar.activation(
+                        out=x_wide[i][:, j * 128 : (j + 1) * 128], in_=src, func=ACT.Copy, scale=xs[:, i, j : j + 1]
+                    )
+
+        def turn_x(i, nbanks):
+            words = x_wide[i][:].bitcast(F32)
+            x_turned[i] = []
+            for half in range(2):
+                b = turn_bank(nbanks, "xT%d_%d" % (i, half))
+                for s in range(4):
+                    g, u = 2 * half + s // 2, s % 2
+                    if i < VECTOR_WIDENS:
+                        src = words[:, 256 * g + 128 * u : 256 * g + 128 * (u + 1)]
+                    else:
+                        src = words[:, 256 * g + u : 256 * (g + 1) : 2]
+                    nc.tensor.transpose(b[:, s, :], src, ident[:])
+                x_turned[i].append(b)
+
+        x_grp = {}
+
+        def evac_x(i):
+            x_grp[i] = work.tile([P, G1 * P * 4], BF16, name="x_grp%d" % i, tag="x_grp", bufs=2, align_bytes=64)
+            for half in range(2):
+                dst = x_grp[i][:, 1024 * half : 1024 * (half + 1)].bitcast(F32).rearrange("p (a r u) -> p a r u", a=2, u=2)
+                nc.scalar.copy(out=dst, in_=x_turned[i][half][:].rearrange("p (a u) r -> p a r u", u=2))
+
+        def quant_x(i, half):
+            if half == 0:
+                x_codes[i] = work.tile([P, G1 * P], U32, name="x_codes%d" % i, tag="x_codes", bufs=5, align_bytes=64)
+                x_scl[i] = work.tile([P, G1 * P], U8, name="x_scl%d" % i, tag="x_scl", bufs=5, align_bytes=64)
+            cols = slice(256 * half, 256 * (half + 1))
+            nc.vector.quantize_mx(out=x_codes[i][:, cols].bitcast(FP8X4), scales=x_scl[i][:, cols], in_=x_grp[i][:, 1024 * half : 1024 * (half + 1)])
+
+        w_turned, w_grp = {}, {}
+
+        def turn_w(q, g):
+            b = turn_bank(4, "wT%d_%d" % (q, g))
+            for s in range(4):
+                a, u = s // 2, s % 2
+                words = w_raw[2 * q + a][:].bitcast(F32)
+                nc.tensor.transpose(b[:, s, :], words[:, 256 * g + u : 256 * (g + 1) : 2], ident[:])
+            w_turned[q, g] = b
+
+        def evac_w(q, g):
+            w_grp[q, g] = work.tile([P, 1024], BF16, name="w_grp%d_%d" % (q, g), tag="w_grp", bufs=4, align_bytes=64)
+            dst = w_grp[q, g][:].bitcast(F32).rearrange("p (a r u) -> p a r u", a=2, u=2)
+            nc.scalar.copy(out=dst, in_=w_turned[q, g][:].rearrange("p (a u) r -> p a r u", u=2))
+
+        def quant_w(q, g):
+            cols = slice(256 * q, 256 * (q + 1))
+            nc.vector.quantize_mx(out=w_codes[:, g, cols].bitcast(FP8X4), scales=w_scale[:, g, cols], in_=w_grp[q, g][:])
+
+        def readout(i, h, k, lo, hi):
+            if (i, h) not in y_acc:
+                y_acc[i, h] = bank(k, [P, 512], F32, "y_acc%d_%d" % (i, h))
+            cols = slice(512 * h + lo, 512 * h + hi)
+            for g in range(G1):
+                nc.tensor.matmul_mx(
+                    out=y_acc[i, h][:, lo:hi],
+                    lhsT=x_codes[i][:, g * P : (g + 1) * P].bitcast(FP8X4), lhsT_scale=x_scl[i][:, g * P : (g + 1) * P],
+                    rhs=w_codes[:, g, cols].bitcast(FP8X4), rhs_scale=w_scale[:, g, cols],
+                    start=(g == 0), stop=(g == G1 - 1),
+                )
+
+        def add_bias(i, h):
+            if h == 0:
+                y_sb[i] = work.tile([P, N], F32, name="y%d" % i, tag="row4k", bufs=TILES)
+            cols = slice(512 * h, 512 * (h + 1))
+            nc.vector.tensor_tensor(out=y_sb[i][:, cols], in0=y_acc[i, h][:], in1=bias[:, cols], op=ALU.add)
+
+        def store_y(i):
+            nc.sync.dma_start(out=out_0[i * P : (i + 1) * P, :], in_=y_sb[i][:])
+
+        def apply_gain(i, h):
+            if h == 0:
+                z_wide[i] = work.tile([P, N], BF16, name="z_wide%d" % i, tag="z_wide", bufs=4)
+            cols = slice(512 * h, 512 * (h + 1))
+            eng = nc.gpsimd if Z_ON_POOL else nc.vector
+            eng.tensor_tensor(
+                out=z_wide[i][:, cols].rearrange("t (u p e) -> t u p e", u=2, e=2),
+                in0=y_sb[i][:, cols].rearrange("t (p u e) -> t u p e", u=2, e=2),
+                in1=gain[:, cols].rearrange("t (u p e) -> t u p e", u=2, e=2),
+                op=ALU.mult,
+            )
+
+        def turn_z(i, nbanks):
+            b = turn_bank(nbanks, "zT%d" % i)
+            words = z_wide[i][:].bitcast(F32)
+            for s in range(4):
+                nc.tensor.transpose(b[:, s, :], words[:, 128 * s : 128 * (s + 1)], ident[:])
+            z_turned[i] = b
+
+        z_grp = {}
+
+        def evac_z(i):
+            z_grp[i] = work.tile([P, 1024], BF16, name="z_grp%d" % i, tag="w_grp", bufs=4, align_bytes=64)
+            dst = z_grp[i][:].bitcast(F32).rearrange("p (a r u) -> p a r u", a=2, u=2)
+            nc.scalar.copy(out=dst, in_=z_turned[i][:].rearrange("p (a u) r -> p a r u", u=2))
+
+        def quant_z(i):
+            z_codes[i] = work.tile([P, G2 * P], U32, name="z_codes%d" % i, tag="z_codes", bufs=3, align_bytes=64)
+            z_scl[i] = work.tile([P, G2 * P], U8, name="z_scl%d" % i, tag="z_scl", bufs=3, align_bytes=64)
+            nc.vector.quantize_mx(out=z_codes[i][:].bitcast(FP8X4), scales=z_scl[i][:], in_=z_grp[i][:])
+
+        def feedback(i, c):
+            f_acc[i, c] = bank(3 + (4 * i + c) % 3, [P, 512], F32, "f_acc%d_%d" % (i, c))
+            for g in range(G2):
+                nc.tensor.matmul_mx(
+                    out=f_acc[i, c][:],
+                    lhsT=z_codes[i][:, g * P : (g + 1) * P].bitcast(FP8X4), lhsT_scale=z_scl[i][:, g * P : (g + 1) * P],
+                    rhs=fb_words[:, g, 1024 * c : 1024 * (c + 1)].bitcast(FP4X4), rhs_scale=fb_scale[:, g, 512 * c : 512 * (c + 1)],
+                    start=(g == 0), stop=(g == G2 - 1),
+                )
+
+        def add_drive(i, c):
+            if c == 0:
+                state[i] = work.tile([P, K], F32, name="state%d" % i, tag="state", bufs=3)
+            cols = slice(512 * c, 512 * (c + 1))
+            nc.vector.tensor_tensor(out=state[i][:, cols], in0=f_acc[i, c][:], in1=drv[i][:, cols], op=ALU.add)
+
+        def finish(i, lo, hi):
+            nc.scalar.activation(out=state[i][:, lo:hi], in_=state[i][:, lo:hi], func=ACT.Tanh)
+            nc.sync.dma_start(out=out_1[i * P : (i + 1) * P, lo:hi], in_=state[i][:, lo:hi])
+
+        def spread_rows():
+            for v, src in enumerate((bias_words, gain_words)):
+                b = bank(6 + v, [P, 4, P], F32, "spread%d" % v)
+                for j in range(4):
+                    nc.tensor.transpose(b[:, j, :], src[:, j : j + 1].to_broadcast([P, P]), ident[:])
+                if v == 0:
+                    nc.scalar.copy(out=bias[:].bitcast(F32).rearrange("t (p j) -> t p j", j=4), in_=b[:].rearrange("t j p -> t p j"))
+                else:
+                    for g in range(G2):
+                        nc.scalar.copy(
+                            out=gain[:, 512 * g : 512 * (g + 1)].bitcast(F32).rearrange("t (u p a) -> t u p a", u=2, a=2),
+                            in_=b[:, :, 64 * g : 64 * (g + 1)].rearrange("t (a u) p -> t u p a", u=2),
+                        )
+
+        def w_quarter(q):
+            for g in range(G1):
+                turn_w(q, g)
+                evac_w(q, g)
+                quant_w(q, g)
+
+        def prepare_x(i, nbanks):
+            turn_x(i, nbanks)
+            evac_x(i)
+            quant_x(i, 0)
+            quant_x(i, 1)
+
+        def prepare_z(i):
+            turn_z(i, 3)
+            evac_z(i)
+            quant_z(i)
+
+        def close_half(i, h):
+            add_bias(i, h)
+            if h == 1:
+                store_y(i)
+            apply_gain(i, h)
+
+        every = range(BLOCKS)
+        spread_rows()
+        widen(0, every)
+        prepare_x(0, 4)
+        w_quarter(0)
+        widen(1, every)
+        prepare_x(1, 4)
+        w_quarter(1)
+        widen(2, every)
+        readout(0, 0, 4, 0, 256)
+        readout(1, 0, 5, 0, 256)
+        w_quarter(2)
+        readout(0, 0, 4, 256, 512)
+        close_half(0, 0)
+        readout(1, 0, 5, 256, 512)
+        close_half(1, 0)
+        prepare_x(2, 4)
+        widen(3, every)
+        w_quarter(3)
+        readout(0, 1, 6, 0, 256)
+        readout(1, 1, 7, 0, 256)
+        readout(2, 0, 4, 0, 512)
+        close_half(2, 0)
+        readout(0, 1, 6, 256, 512)
+        close_half(0, 1)
+        readout(1, 1, 7, 256, 512)
+        close_half(1, 1)
+        prepare_x(3, 4)
+        widen(4, every)
+        prepare_z(0)
+        readout(2, 1, 5, 0, 512)
+        close_half(2, 1)
+
+        for j in range(TILES):
+            last = j == TILES - 1
+            if j + 4 < TILES:
+                prepare_x(j + 4, 3)
+            if j + 1 < TILES:
+                prepare_z(j + 1)
+            if j + 5 < TILES:
+                widen(j + 5, every)
+            for h in range(2):
+                for c in (2 * h, 2 * h + 1):
+                    feedback(j, c)
+                    add_drive(j, c)
+                    if last:
+                        finish(j, 512 * c, 512 * (c + 1))
+                if not last:
+                    finish(j, 1024 * h, 1024 * (h + 1))
+                if j + 3 < TILES:
+                    readout(j + 3, h, 6 + h, 0, 512)
+                    close_half(j + 3, h)

@@ -52,6 +52,8 @@ def tile_reservoir_readout_feedback_d4_kernel(
         w_scale = keep.tile([P, G1, N], U8, name="w_scale", align_bytes=64)
         xs = keep.tile([P, TILES, BLOCKS], F32, name="xs")
 
+        idle = keep.tile([P, 512], BF16, name="idle")
+        nc.vector.memset(idle[:].bitcast(I32), 0)
         nc.vector.memset(warm[:], 0.0)
         make_identity(nc, ident[:])
         nc.gpsimd.memset(fb_scale[:].rearrange("p g n -> p (g n)").bitcast(I32), 0)
@@ -253,8 +255,15 @@ def tile_reservoir_readout_feedback_d4_kernel(
                             in_=b[:, :, 64 * g : 64 * (g + 1)].rearrange("t (a u) p -> t u p a", u=2),
                         )
 
+        def keep_busy(count, width):
+            b = bank(0, [P, 512], F32, "unused")
+            for n in range(count):
+                nc.tensor.matmul(b[:, 0:width], idle[:, 0:P], idle[:, 0:width], start=True, stop=True)
+
         def w_quarter(q):
             for g in range(G1):
+                if g == 2:
+                    keep_busy(1, 256)
                 turn_w(q, g)
                 evac_w(q, g)
                 quant_w(q, g)
@@ -277,34 +286,37 @@ def tile_reservoir_readout_feedback_d4_kernel(
             apply_gain(i, h)
 
         every = range(BLOCKS)
+        keep_busy(6, 512)
         spread_rows()
+        keep_busy(1, 512)
         widen(0, every)
         prepare_x(0, 4)
-        w_quarter(0)
+        keep_busy(1, 512)
         widen(1, every)
+        w_quarter(0)
+        keep_busy(1, 256)
         prepare_x(1, 4)
+        keep_busy(1, 256)
         w_quarter(1)
-        widen(2, every)
         readout(0, 0, 4, 0, 256)
         readout(1, 0, 5, 0, 256)
         w_quarter(2)
-        readout(0, 0, 4, 256, 512)
-        close_half(0, 0)
-        readout(1, 0, 5, 256, 512)
-        close_half(1, 0)
-        prepare_x(2, 4)
-        widen(3, every)
+        widen(2, every)
+        for i in range(2):
+            readout(i, 0, 4, 256, 512)
+            close_half(i, 0)
         w_quarter(3)
+        widen(3, every)
         readout(0, 1, 6, 0, 256)
         readout(1, 1, 7, 0, 256)
-        readout(2, 0, 4, 0, 512)
-        close_half(2, 0)
-        readout(0, 1, 6, 256, 512)
-        close_half(0, 1)
-        readout(1, 1, 7, 256, 512)
-        close_half(1, 1)
+        prepare_x(2, 4)
+        for i in range(2):
+            readout(i, 1, 4, 256, 512)
+            close_half(i, 1)
         prepare_x(3, 4)
         widen(4, every)
+        readout(2, 0, 4, 0, 512)
+        close_half(2, 0)
         prepare_z(0)
         readout(2, 1, 5, 0, 512)
         close_half(2, 1)

@@ -23,7 +23,7 @@ G1 = K // 512
 G2 = N // 512
 BLOCKS = K // 128
 QUARTERS = 4
-VECTOR_WIDENS = 5
+VECTOR_WIDENS = 4
 Z_ON_POOL = False
 
 
@@ -78,12 +78,13 @@ def tile_reservoir_readout_feedback_d4_kernel(
         load_w(1)
         nc.sync.dma_start(out=xs[:, 1:, :], in_=scale_rows[:, 1:, :])
         load_x(1)
-        load_w(2)
-        load_w(3)
-        load_x(2)
-        for r in range(4, 8):
+        for r in range(2, 6):
             load_w(r)
+        load_x(2)
+        load_w(6)
+        load_w(7)
         load_x(3)
+        load_x(4)
         for q in range(4):
             nc.sync.dma_start(
                 out=fb_scale[32 * q : 32 * q + 4, :, :].bitcast(I32),
@@ -93,8 +94,8 @@ def tile_reservoir_readout_feedback_d4_kernel(
             nc.sync.dma_start(out=fb_words[:, g, :].bitcast(I32), in_=w_fb_words[g].bitcast(I32))
         for i in range(TILES):
             nc.sync.dma_start(out=drv[i][:], in_=drive[i * P : (i + 1) * P, :])
-            if 4 + i < TILES:
-                load_x(4 + i)
+            if 5 + i < TILES:
+                load_x(5 + i)
 
         x_wide, x_turned, x_codes, x_scl = {}, {}, {}, {}
         y_acc, y_sb, z_wide, z_turned, z_codes, z_scl, f_acc, state = {}, {}, {}, {}, {}, {}, {}, {}
@@ -110,11 +111,8 @@ def tile_reservoir_readout_feedback_d4_kernel(
             for j in blocks:
                 src = x8[i][:, j * 128 : (j + 1) * 128].bitcast(FP8)
                 if i < VECTOR_WIDENS:
-                    g, q = divmod(j, 4)
-                    dst = x_wide[i][:].rearrange("t (g u p e) -> t g p u e", g=G1, u=2, e=2)[:, g, 32 * q : 32 * q + 32]
                     nc.vector.tensor_scalar(
-                        out=dst, in0=src.rearrange("t (p u e) -> t p u e", u=2, e=2),
-                        scalar1=xs[:, i, j : j + 1], scalar2=None, op0=ALU.mult,
+                        out=x_wide[i][:, j * 128 : (j + 1) * 128], in0=src, scalar1=xs[:, i, j : j + 1], scalar2=None, op0=ALU.mult
                     )
                 else:
                     nc.scalar.activation(
@@ -128,10 +126,7 @@ def tile_reservoir_readout_feedback_d4_kernel(
                 b = turn_bank(nbanks, "xT%d_%d" % (i, half))
                 for s in range(4):
                     g, u = 2 * half + s // 2, s % 2
-                    if i < VECTOR_WIDENS:
-                        src = words[:, 256 * g + 128 * u : 256 * g + 128 * (u + 1)]
-                    else:
-                        src = words[:, 256 * g + u : 256 * (g + 1) : 2]
+                    src = words[:, 256 * g + u : 256 * (g + 1) : 2]
                     nc.tensor.transpose(b[:, s, :], src, ident[:])
                 x_turned[i].append(b)
 
@@ -262,8 +257,6 @@ def tile_reservoir_readout_feedback_d4_kernel(
 
         def w_quarter(q):
             for g in range(G1):
-                if g == 2:
-                    keep_busy(1, 256)
                 turn_w(q, g)
                 evac_w(q, g)
                 quant_w(q, g)
@@ -294,9 +287,9 @@ def tile_reservoir_readout_feedback_d4_kernel(
         keep_busy(1, 512)
         widen(1, every)
         w_quarter(0)
-        keep_busy(1, 256)
+        keep_busy(1, 512)
         prepare_x(1, 4)
-        keep_busy(1, 256)
+        keep_busy(1, 512)
         w_quarter(1)
         readout(0, 0, 4, 0, 256)
         readout(1, 0, 5, 0, 256)

@@ -4,7 +4,7 @@ import concourse.mybir as mybir
 from concourse.masks import make_identity
 
 T, K, N = 1024, 2048, 1024
-FLOPS = 2 * T * K * N * 2
+FLOPS = 2 * (2 * T * K * N)
 
 F32 = mybir.dt.float32
 BF16 = mybir.dt.bfloat16
@@ -18,13 +18,17 @@ ALU = mybir.AluOpType
 ACT = mybir.ActivationFunctionType
 
 P = 128
+PASS = 512
+BANK = 512
 TILES = T // P
-G1 = K // 512
-G2 = N // 512
-BLOCKS = K // 128
-QUARTERS = 4
-VECTOR_WIDENS = 4
-Z_ON_POOL = False
+W_TILES = N // P
+PASSES_1 = K // PASS
+PASSES_2 = N // PASS
+SCALE_RUN = 128
+QUARTER = 256
+CHUNKS = K // BANK
+SCALAR_TILES = (4, 5)
+LEAD = 3
 
 
 def tile_reservoir_readout_feedback_d4_kernel(
@@ -35,47 +39,51 @@ def tile_reservoir_readout_feedback_d4_kernel(
         keep = ctx.enter_context(tc.tile_pool(name="keep", bufs=1))
         work = ctx.enter_context(tc.tile_pool(name="work", bufs=2))
         psum = ctx.enter_context(tc.psum_pool(name="psum", bufs=8))
-        ctx.enter_context(tc.manual_schedule(engines={mybir.EngineType.PE}))
+        ctx.enter_context(tc.manual_schedule())
 
-        def bank(k, shape, dtype, name):
-            return psum.tile(shape, dtype, name=name, tag="bank")
+        def bank(shape, name):
+            return psum.tile(shape, F32, name=name, tag="bank")
+
+        def rows(i):
+            return slice(i * P, (i + 1) * P)
+
+        def part(n, width):
+            return slice(n * width, (n + 1) * width)
 
         ident = keep.tile([P, P], F32, name="ident")
-        bias_words = keep.tile([P, 4], F32, name="bias_words")
-        gain_words = keep.tile([P, 4], F32, name="gain_words")
-        warm = keep.tile([P, 1], F32, name="warm")
-        fb_scale = keep.tile([P, G2, K], U8, name="fb_scale", align_bytes=64)
-        fb_words = keep.tile([P, G2, 2 * K], U8, name="fb_words", align_bytes=64)
+        table_probe = keep.tile([P, 1], F32, name="table_probe")
+        bias_pairs = keep.tile([P, 4], F32, name="bias_pairs")
+        gain_pairs = keep.tile([P, 4], F32, name="gain_pairs")
         bias = keep.tile([P, N], BF16, name="bias")
         gain = keep.tile([P, N], BF16, name="gain")
-        w_codes = keep.tile([P, G1, N], U32, name="w_codes", align_bytes=64)
-        w_scale = keep.tile([P, G1, N], U8, name="w_scale", align_bytes=64)
-        xs = keep.tile([P, TILES, BLOCKS], F32, name="xs")
-
-        idle = keep.tile([P, 512], BF16, name="idle")
-        nc.vector.memset(idle[:].bitcast(I32), 0)
-        nc.vector.memset(warm[:], 0.0)
-        make_identity(nc, ident[:])
-        nc.gpsimd.memset(fb_scale[:].rearrange("p g n -> p (g n)").bitcast(I32), 0)
-        nc.scalar.activation(out=warm[:], in_=warm[:], func=ACT.Tanh)
-
+        xs = keep.tile([P, TILES, K // SCALE_RUN], F32, name="xs")
+        w_codes = keep.tile([P, PASSES_1, N], U32, name="w_codes", align_bytes=64)
+        w_scales = keep.tile([P, PASSES_1, N], U8, name="w_scales", align_bytes=64)
+        fb_words = keep.tile([P, PASSES_2, 2 * K], U8, name="fb_words", align_bytes=64)
+        fb_scales = keep.tile([P, PASSES_2, K], U8, name="fb_scales", align_bytes=64)
         x8 = [keep.tile([P, K], U8, name="xbytes%d" % i) for i in range(TILES)]
-        w_raw = [work.tile([P, K], BF16, name="w_raw%d" % r, tag="row4k", bufs=TILES) for r in range(TILES)]
-        drv = [keep.tile([P, K], BF16, name="drv%d" % i) for i in range(TILES)]
+        drv = [keep.tile([P, K], BF16, name="drive%d" % i) for i in range(TILES)]
+        w_raw = [work.tile([P, K], BF16, name="w_raw%d" % r, tag="rows", bufs=W_TILES) for r in range(W_TILES)]
+
+        make_identity(nc, ident[:])
+        nc.gpsimd.memset(fb_scales[:].rearrange("p g n -> p (g n)").bitcast(I32), 0)
+        nc.vector.memset(table_probe[:], 0.0)
+        nc.scalar.activation(out=table_probe[:], in_=table_probe[:], func=ACT.Tanh)
 
         def load_x(i):
-            nc.sync.dma_start(out=x8[i][:], in_=x_bytes[i * P : (i + 1) * P, :])
+            nc.sync.dma_start(out=x8[i][:], in_=x_bytes[rows(i), :])
 
-        def load_w(r):
-            nc.sync.dma_start(out=w_raw[r][:], in_=w_out[r * P : (r + 1) * P, :])
+        def load_w(r, cols=slice(0, K)):
+            nc.sync.dma_start(out=w_raw[r][:, cols], in_=w_out[rows(r), cols])
 
         scale_rows = x_scale.rearrange("(i p) j -> p i j", p=P)
+        nc.sync.dma_start(out=bias_pairs[:].bitcast(BF16), in_=b_out.rearrange("(p j) -> p j", p=P))
+        nc.sync.dma_start(out=gain_pairs[:].bitcast(BF16), in_=fb_gain.rearrange("(p j) -> p j", p=P))
         nc.sync.dma_start(out=xs[:, 0, :], in_=scale_rows[:, 0, :])
         load_x(0)
-        nc.sync.dma_start(out=bias_words[:].bitcast(BF16), in_=b_out.rearrange("(p j) -> p j", p=P))
-        nc.sync.dma_start(out=gain_words[:].bitcast(BF16), in_=fb_gain.rearrange("(p j) -> p j", p=P))
-        load_w(0)
-        load_w(1)
+        for half in range(2):
+            load_w(0, part(half, K // 2))
+            load_w(1, part(half, K // 2))
         nc.sync.dma_start(out=xs[:, 1:, :], in_=scale_rows[:, 1:, :])
         load_x(1)
         for r in range(2, 6):
@@ -85,251 +93,339 @@ def tile_reservoir_readout_feedback_d4_kernel(
         load_w(7)
         load_x(3)
         load_x(4)
-        for q in range(4):
+        for quadrant in range(4):
             nc.sync.dma_start(
-                out=fb_scale[32 * q : 32 * q + 4, :, :].bitcast(I32),
-                in_=w_fb_scales[:, 4 * q : 4 * q + 4, :].rearrange("g r n -> r g n").bitcast(I32),
+                out=fb_scales[32 * quadrant : 32 * quadrant + 4, :, :].bitcast(I32),
+                in_=w_fb_scales[:, part(quadrant, 4), :].rearrange("g r n -> r g n").bitcast(I32),
             )
-        for g in range(G2):
+        for g in range(PASSES_2):
             nc.sync.dma_start(out=fb_words[:, g, :].bitcast(I32), in_=w_fb_words[g].bitcast(I32))
         for i in range(TILES):
-            nc.sync.dma_start(out=drv[i][:], in_=drive[i * P : (i + 1) * P, :])
-            if 5 + i < TILES:
-                load_x(5 + i)
+            nc.sync.dma_start(out=drv[i][:], in_=drive[rows(i), :])
+            if i + 5 < TILES:
+                load_x(i + 5)
 
-        x_wide, x_turned, x_codes, x_scl = {}, {}, {}, {}
-        y_acc, y_sb, z_wide, z_turned, z_codes, z_scl, f_acc, state = {}, {}, {}, {}, {}, {}, {}, {}
-        turn_count = [0]
+        def to_split_order(copy, dst, src):
+            copy(
+                out=dst.bitcast(F32).rearrange("t (g u p) -> t g u p", u=2, p=P),
+                in_=src.bitcast(F32).rearrange("t (g p u) -> t g u p", u=2, p=P),
+            )
 
-        def turn_bank(nbanks, name):
-            turn_count[0] += 1
-            return bank(turn_count[0] % nbanks, [P, 4, P], F32, name)
+        def turn(sources, name):
+            turned = bank([P, 4, P], name)
+            for slot, src in enumerate(sources):
+                nc.tensor.transpose(turned[:, slot, :], src, ident[:])
+            return turned
 
-        def widen(i, blocks):
-            if i not in x_wide:
-                x_wide[i] = work.tile([P, K], BF16, name="x_wide%d" % i, tag="x_wide", bufs=4)
-            for j in blocks:
-                src = x8[i][:, j * 128 : (j + 1) * 128].bitcast(FP8)
-                if i < VECTOR_WIDENS:
-                    nc.vector.tensor_scalar(
-                        out=x_wide[i][:, j * 128 : (j + 1) * 128], in0=src, scalar1=xs[:, i, j : j + 1], scalar2=None, op0=ALU.mult
-                    )
-                else:
-                    nc.scalar.activation(
-                        out=x_wide[i][:, j * 128 : (j + 1) * 128], in_=src, func=ACT.Copy, scale=xs[:, i, j : j + 1]
-                    )
+        def interleave(dst, turned):
+            nc.scalar.copy(
+                out=dst.bitcast(F32).rearrange("p (a r u) -> p a r u", a=2, u=2),
+                in_=turned[:].rearrange("p (a u) r -> p a r u", u=2),
+            )
 
-        def turn_x(i, nbanks):
-            words = x_wide[i][:].bitcast(F32)
-            x_turned[i] = []
-            for half in range(2):
-                b = turn_bank(nbanks, "xT%d_%d" % (i, half))
-                for s in range(4):
-                    g, u = 2 * half + s // 2, s % 2
-                    src = words[:, 256 * g + u : 256 * (g + 1) : 2]
-                    nc.tensor.transpose(b[:, s, :], src, ident[:])
-                x_turned[i].append(b)
+        def spread(pairs, name):
+            return turn([pairs[:, j : j + 1].to_broadcast([P, P]) for j in range(4)], name)
 
-        x_grp = {}
-
-        def evac_x(i):
-            x_grp[i] = work.tile([P, G1 * P * 4], BF16, name="x_grp%d" % i, tag="x_grp", bufs=2, align_bytes=64)
-            for half in range(2):
-                dst = x_grp[i][:, 1024 * half : 1024 * (half + 1)].bitcast(F32).rearrange("p (a r u) -> p a r u", a=2, u=2)
-                nc.scalar.copy(out=dst, in_=x_turned[i][half][:].rearrange("p (a u) r -> p a r u", u=2))
-
-        def quant_x(i, half):
-            if half == 0:
-                x_codes[i] = work.tile([P, G1 * P], U32, name="x_codes%d" % i, tag="x_codes", bufs=5, align_bytes=64)
-                x_scl[i] = work.tile([P, G1 * P], U8, name="x_scl%d" % i, tag="x_scl", bufs=5, align_bytes=64)
-            cols = slice(256 * half, 256 * (half + 1))
-            nc.vector.quantize_mx(out=x_codes[i][:, cols].bitcast(FP8X4), scales=x_scl[i][:, cols], in_=x_grp[i][:, 1024 * half : 1024 * (half + 1)])
-
-        w_turned, w_grp = {}, {}
-
-        def turn_w(q, g):
-            b = turn_bank(4, "wT%d_%d" % (q, g))
-            for s in range(4):
-                a, u = s // 2, s % 2
-                words = w_raw[2 * q + a][:].bitcast(F32)
-                nc.tensor.transpose(b[:, s, :], words[:, 256 * g + u : 256 * (g + 1) : 2], ident[:])
-            w_turned[q, g] = b
-
-        def evac_w(q, g):
-            w_grp[q, g] = work.tile([P, 1024], BF16, name="w_grp%d_%d" % (q, g), tag="w_grp", bufs=4, align_bytes=64)
-            dst = w_grp[q, g][:].bitcast(F32).rearrange("p (a r u) -> p a r u", a=2, u=2)
-            nc.scalar.copy(out=dst, in_=w_turned[q, g][:].rearrange("p (a u) r -> p a r u", u=2))
-
-        def quant_w(q, g):
-            cols = slice(256 * q, 256 * (q + 1))
-            nc.vector.quantize_mx(out=w_codes[:, g, cols].bitcast(FP8X4), scales=w_scale[:, g, cols], in_=w_grp[q, g][:])
-
-        def readout(i, h, k, lo, hi):
-            if (i, h) not in y_acc:
-                y_acc[i, h] = bank(k, [P, 512], F32, "y_acc%d_%d" % (i, h))
-            cols = slice(512 * h + lo, 512 * h + hi)
-            for g in range(G1):
-                nc.tensor.matmul_mx(
-                    out=y_acc[i, h][:, lo:hi],
-                    lhsT=x_codes[i][:, g * P : (g + 1) * P].bitcast(FP8X4), lhsT_scale=x_scl[i][:, g * P : (g + 1) * P],
-                    rhs=w_codes[:, g, cols].bitcast(FP8X4), rhs_scale=w_scale[:, g, cols],
-                    start=(g == 0), stop=(g == G1 - 1),
+        def spread_bias_and_gain():
+            nc.scalar.copy(
+                out=bias[:].bitcast(F32).rearrange("t (p j) -> t p j", j=4),
+                in_=spread(bias_pairs, "bias_spread")[:].rearrange("t j p -> t p j"),
+            )
+            spread_gain = spread(gain_pairs, "gain_spread")
+            for h in range(PASSES_2):
+                nc.scalar.copy(
+                    out=gain[:, part(h, PASS)].bitcast(F32).rearrange("t (u c a) -> t u c a", u=2, a=2),
+                    in_=spread_gain[:, :, part(h, P // 2)].rearrange("t (a u) c -> t u c a", u=2),
                 )
+
+        x_split, x_plain, x_turned, x_grouped, x_codes, x_scales = {}, {}, {}, {}, {}, {}
+
+        def split_tile(name):
+            return work.tile([P, K], BF16, name=name, tag="split", bufs=6)
+
+        def scaled_run(i, j):
+            return x8[i][:, part(j, SCALE_RUN)].bitcast(FP8), xs[:, i, j : j + 1]
+
+        def widen_on_vector(i, passes):
+            if i not in x_split:
+                x_split[i] = split_tile("x_split%d" % i)
+            by_pair = x_split[i][:].rearrange("t (g u p e) -> t g p u e", g=PASSES_1, u=2, e=2)
+            for g in passes:
+                for q in range(4):
+                    codes, scale = scaled_run(i, 4 * g + q)
+                    nc.vector.tensor_scalar(
+                        out=by_pair[:, g, part(q, 32)],
+                        in0=codes.rearrange("t (p u e) -> t p u e", u=2, e=2),
+                        scalar1=scale,
+                        scalar2=None,
+                        op0=ALU.mult,
+                    )
+
+        def widen_on_scalar(i, half):
+            if half == 0:
+                x_split[i] = split_tile("x_split%d" % i)
+                x_plain[i] = work.tile([P, K], BF16, name="x_plain%d" % i, tag="x_plain")
+            for j in range(8 * half, 8 * half + 8):
+                codes, scale = scaled_run(i, j)
+                nc.scalar.activation(out=x_plain[i][:, part(j, SCALE_RUN)], in_=codes, func=ACT.Copy, scale=scale)
+            cols = part(half, K // 2)
+            to_split_order(nc.scalar.copy, x_split[i][:, cols], x_plain[i][:, cols])
+
+        def turn_x(i):
+            pairs = x_split[i][:].bitcast(F32)
+            for half in range(2):
+                x_turned[i, half] = turn([pairs[:, part(4 * half + s, P)] for s in range(4)], "xT%d_%d" % (i, half))
+
+        def empty_x(i):
+            x_grouped[i] = work.tile([P, K], BF16, name="x_grouped%d" % i, tag="x_grouped", align_bytes=64)
+            for half in range(2):
+                interleave(x_grouped[i][:, part(half, K // 2)], x_turned[i, half])
+
+        def quantise_x(i, half):
+            if half == 0:
+                x_codes[i] = work.tile([P, PASSES_1 * P], U32, name="x_codes%d" % i, tag="x_codes", bufs=5, align_bytes=64)
+                x_scales[i] = work.tile([P, PASSES_1 * P], U8, name="x_scales%d" % i, tag="x_scales", bufs=5, align_bytes=64)
+            cols = part(half, 2 * P)
+            nc.vector.quantize_mx(
+                out=x_codes[i][:, cols].bitcast(FP8X4), scales=x_scales[i][:, cols], in_=x_grouped[i][:, part(half, K // 2)]
+            )
+
+        w_split, w_turned, w_grouped = {}, {}, {}
+
+        def grouped_tile(name):
+            return work.tile([P, 4 * QUARTER], BF16, name=name, tag="grouped", bufs=6, align_bytes=64)
+
+        def split_w(r, copy):
+            w_split[r] = split_tile("w_split%d" % r)
+            to_split_order(copy, w_split[r][:], w_raw[r][:])
+
+        def w_pairs(r, g, u):
+            if r in w_split:
+                return w_split[r][:].bitcast(F32)[:, part(2 * g + u, P)]
+            return w_raw[r][:].bitcast(F32)[:, 2 * P * g + u : 2 * P * (g + 1) : 2]
+
+        def turn_w(q):
+            for g in range(PASSES_1):
+                w_turned[q, g] = turn([w_pairs(2 * q + a, g, u) for a in range(2) for u in range(2)], "wT%d_%d" % (q, g))
+
+        def empty_w(q, passes):
+            for g in passes:
+                w_grouped[q, g] = grouped_tile("w_grouped%d_%d" % (q, g))
+                interleave(w_grouped[q, g][:], w_turned[q, g])
+
+        def quantise_w(q, passes):
+            for g in passes:
+                cols = part(q, QUARTER)
+                nc.vector.quantize_mx(out=w_codes[:, g, cols].bitcast(FP8X4), scales=w_scales[:, g, cols], in_=w_grouped[q, g][:])
+
+        y_sum, y_sb, z_split, z_turned, z_grouped, z_codes, z_scales = {}, {}, {}, {}, {}, {}, {}
+
+        def readout(i, first, width):
+            h, offset = divmod(first, BANK)
+            if offset == 0:
+                y_sum[i, h] = bank([P, BANK], "y_sum%d_%d" % (i, h))
+            cols = slice(first, first + width)
+            for g in range(PASSES_1):
+                nc.tensor.matmul_mx(
+                    out=y_sum[i, h][:, offset : offset + width],
+                    lhsT=x_codes[i][:, part(g, P)].bitcast(FP8X4),
+                    lhsT_scale=x_scales[i][:, part(g, P)],
+                    rhs=w_codes[:, g, cols].bitcast(FP8X4),
+                    rhs_scale=w_scales[:, g, cols],
+                    start=(g == 0),
+                    stop=(g == PASSES_1 - 1),
+                )
+
+        def readout_quarter(i, q):
+            readout(i, q * QUARTER, QUARTER)
+
+        def readout_half(i, h):
+            readout(i, h * BANK, BANK)
 
         def add_bias(i, h):
             if h == 0:
-                y_sb[i] = work.tile([P, N], F32, name="y%d" % i, tag="row4k", bufs=TILES)
-            cols = slice(512 * h, 512 * (h + 1))
-            nc.vector.tensor_tensor(out=y_sb[i][:, cols], in0=y_acc[i, h][:], in1=bias[:, cols], op=ALU.add)
-
-        def store_y(i):
-            nc.sync.dma_start(out=out_0[i * P : (i + 1) * P, :], in_=y_sb[i][:])
+                y_sb[i] = work.tile([P, N], F32, name="y%d" % i, tag="rows", bufs=W_TILES)
+            cols = part(h, BANK)
+            nc.vector.tensor_tensor(out=y_sb[i][:, cols], in0=y_sum[i, h][:], in1=bias[:, cols], op=ALU.add)
+            if h == 1:
+                nc.sync.dma_start(out=out_0[rows(i), :], in_=y_sb[i][:])
 
         def apply_gain(i, h):
             if h == 0:
-                z_wide[i] = work.tile([P, N], BF16, name="z_wide%d" % i, tag="z_wide", bufs=4)
-            cols = slice(512 * h, 512 * (h + 1))
-            eng = nc.gpsimd if Z_ON_POOL else nc.vector
-            eng.tensor_tensor(
-                out=z_wide[i][:, cols].rearrange("t (u p e) -> t u p e", u=2, e=2),
+                z_split[i] = work.tile([P, N], BF16, name="z_split%d" % i, tag="z_split", bufs=4)
+            cols = part(h, PASS)
+            nc.vector.tensor_tensor(
+                out=z_split[i][:, cols].rearrange("t (u p e) -> t u p e", u=2, e=2),
                 in0=y_sb[i][:, cols].rearrange("t (p u e) -> t u p e", u=2, e=2),
                 in1=gain[:, cols].rearrange("t (u p e) -> t u p e", u=2, e=2),
                 op=ALU.mult,
             )
 
-        def turn_z(i, nbanks):
-            b = turn_bank(nbanks, "zT%d" % i)
-            words = z_wide[i][:].bitcast(F32)
-            for s in range(4):
-                nc.tensor.transpose(b[:, s, :], words[:, 128 * s : 128 * (s + 1)], ident[:])
-            z_turned[i] = b
+        def turn_z(i):
+            pairs = z_split[i][:].bitcast(F32)
+            z_turned[i] = turn([pairs[:, part(s, P)] for s in range(4)], "zT%d" % i)
 
-        z_grp = {}
+        def empty_z(i):
+            z_grouped[i] = grouped_tile("z_grouped%d" % i)
+            interleave(z_grouped[i][:], z_turned[i])
 
-        def evac_z(i):
-            z_grp[i] = work.tile([P, 1024], BF16, name="z_grp%d" % i, tag="w_grp", bufs=4, align_bytes=64)
-            dst = z_grp[i][:].bitcast(F32).rearrange("p (a r u) -> p a r u", a=2, u=2)
-            nc.scalar.copy(out=dst, in_=z_turned[i][:].rearrange("p (a u) r -> p a r u", u=2))
+        def quantise_z(i):
+            z_codes[i] = work.tile([P, PASSES_2 * P], U32, name="z_codes%d" % i, tag="z_codes", bufs=3, align_bytes=64)
+            z_scales[i] = work.tile([P, PASSES_2 * P], U8, name="z_scales%d" % i, tag="z_scales", bufs=3, align_bytes=64)
+            nc.vector.quantize_mx(out=z_codes[i][:].bitcast(FP8X4), scales=z_scales[i][:], in_=z_grouped[i][:])
 
-        def quant_z(i):
-            z_codes[i] = work.tile([P, G2 * P], U32, name="z_codes%d" % i, tag="z_codes", bufs=3, align_bytes=64)
-            z_scl[i] = work.tile([P, G2 * P], U8, name="z_scl%d" % i, tag="z_scl", bufs=3, align_bytes=64)
-            nc.vector.quantize_mx(out=z_codes[i][:].bitcast(FP8X4), scales=z_scl[i][:], in_=z_grp[i][:])
+        f_sum, state = {}, {}
 
         def feedback(i, c):
-            f_acc[i, c] = bank(3 + (4 * i + c) % 3, [P, 512], F32, "f_acc%d_%d" % (i, c))
-            for g in range(G2):
+            f_sum[i, c] = bank([P, BANK], "f_sum%d_%d" % (i, c))
+            for g in range(PASSES_2):
                 nc.tensor.matmul_mx(
-                    out=f_acc[i, c][:],
-                    lhsT=z_codes[i][:, g * P : (g + 1) * P].bitcast(FP8X4), lhsT_scale=z_scl[i][:, g * P : (g + 1) * P],
-                    rhs=fb_words[:, g, 1024 * c : 1024 * (c + 1)].bitcast(FP4X4), rhs_scale=fb_scale[:, g, 512 * c : 512 * (c + 1)],
-                    start=(g == 0), stop=(g == G2 - 1),
+                    out=f_sum[i, c][:],
+                    lhsT=z_codes[i][:, part(g, P)].bitcast(FP8X4),
+                    lhsT_scale=z_scales[i][:, part(g, P)],
+                    rhs=fb_words[:, g, part(c, 2 * BANK)].bitcast(FP4X4),
+                    rhs_scale=fb_scales[:, g, part(c, BANK)],
+                    start=(g == 0),
+                    stop=(g == PASSES_2 - 1),
                 )
 
         def add_drive(i, c):
             if c == 0:
                 state[i] = work.tile([P, K], F32, name="state%d" % i, tag="state", bufs=3)
-            cols = slice(512 * c, 512 * (c + 1))
-            nc.vector.tensor_tensor(out=state[i][:, cols], in0=f_acc[i, c][:], in1=drv[i][:, cols], op=ALU.add)
+            cols = part(c, BANK)
+            nc.vector.tensor_tensor(out=state[i][:, cols], in0=f_sum[i, c][:], in1=drv[i][:, cols], op=ALU.add)
 
-        def finish(i, lo, hi):
-            nc.scalar.activation(out=state[i][:, lo:hi], in_=state[i][:, lo:hi], func=ACT.Tanh)
-            nc.sync.dma_start(out=out_1[i * P : (i + 1) * P, lo:hi], in_=state[i][:, lo:hi])
+        def finish(i, cols):
+            nc.scalar.activation(out=state[i][:, cols], in_=state[i][:, cols], func=ACT.Tanh)
+            nc.sync.dma_start(out=out_1[rows(i), cols], in_=state[i][:, cols])
 
-        def spread_rows():
-            for v, src in enumerate((bias_words, gain_words)):
-                b = bank(6 + v, [P, 4, P], F32, "spread%d" % v)
-                for j in range(4):
-                    nc.tensor.transpose(b[:, j, :], src[:, j : j + 1].to_broadcast([P, P]), ident[:])
-                if v == 0:
-                    nc.scalar.copy(out=bias[:].bitcast(F32).rearrange("t (p j) -> t p j", j=4), in_=b[:].rearrange("t j p -> t p j"))
-                else:
-                    for g in range(G2):
-                        nc.scalar.copy(
-                            out=gain[:, 512 * g : 512 * (g + 1)].bitcast(F32).rearrange("t (u p a) -> t u p a", u=2, a=2),
-                            in_=b[:, :, 64 * g : 64 * (g + 1)].rearrange("t (a u) p -> t u p a", u=2),
-                        )
+        def finish_half(i, h):
+            if i + LEAD < TILES:
+                finish(i, part(h, 2 * BANK))
+            else:
+                finish(i, part(2 * h, BANK))
+                finish(i, part(2 * h + 1, BANK))
 
-        def keep_busy(count, width):
-            b = bank(0, [P, 512], F32, "unused")
-            for n in range(count):
-                nc.tensor.matmul(b[:, 0:width], idle[:, 0:P], idle[:, 0:width], start=True, stop=True)
+        every_pass = range(PASSES_1)
+        spread_bias_and_gain()
+        widen_on_vector(0, every_pass)
+        turn_x(0)
+        empty_x(0)
+        quantise_x(0, 0)
+        widen_on_vector(1, [0])
+        quantise_x(0, 1)
+        widen_on_vector(1, [1, 2, 3])
 
-        def w_quarter(q):
-            for g in range(G1):
-                turn_w(q, g)
-                evac_w(q, g)
-                quant_w(q, g)
+        turn_w(0)
+        empty_w(0, every_pass)
+        quantise_w(0, every_pass)
+        turn_x(1)
+        empty_x(1)
+        quantise_x(1, 0)
+        split_w(4, nc.vector.tensor_copy)
+        quantise_x(1, 1)
 
-        def prepare_x(i, nbanks):
-            turn_x(i, nbanks)
-            evac_x(i)
-            quant_x(i, 0)
-            quant_x(i, 1)
+        turn_w(1)
+        empty_w(1, [0, 1])
+        split_w(5, nc.scalar.copy)
+        empty_w(1, [2, 3])
+        split_w(7, nc.scalar.copy)
+        quantise_w(1, [0, 1])
+        widen_on_vector(2, [0, 1])
+        split_w(6, nc.vector.tensor_copy)
+        quantise_w(1, [2, 3])
+        widen_on_vector(2, [2, 3])
+        widen_on_vector(3, [0, 1])
+        readout_quarter(0, 0)
+        readout_quarter(1, 0)
 
-        def prepare_z(i):
-            turn_z(i, 3)
-            evac_z(i)
-            quant_z(i)
-
-        def close_half(i, h):
-            add_bias(i, h)
-            if h == 1:
-                store_y(i)
-            apply_gain(i, h)
-
-        every = range(BLOCKS)
-        keep_busy(6, 512)
-        spread_rows()
-        keep_busy(1, 512)
-        widen(0, every)
-        prepare_x(0, 4)
-        keep_busy(1, 512)
-        widen(1, every)
-        w_quarter(0)
-        keep_busy(1, 512)
-        prepare_x(1, 4)
-        keep_busy(1, 512)
-        w_quarter(1)
-        readout(0, 0, 4, 0, 256)
-        readout(1, 0, 5, 0, 256)
-        w_quarter(2)
-        widen(2, every)
+        turn_w(2)
+        empty_w(2, every_pass)
+        readout_quarter(0, 1)
+        readout_quarter(1, 1)
         for i in range(2):
-            readout(i, 0, 4, 256, 512)
-            close_half(i, 0)
-        w_quarter(3)
-        widen(3, every)
-        readout(0, 1, 6, 0, 256)
-        readout(1, 1, 7, 0, 256)
-        prepare_x(2, 4)
-        for i in range(2):
-            readout(i, 1, 4, 256, 512)
-            close_half(i, 1)
-        prepare_x(3, 4)
-        widen(4, every)
-        readout(2, 0, 4, 0, 512)
-        close_half(2, 0)
-        prepare_z(0)
-        readout(2, 1, 5, 0, 512)
-        close_half(2, 1)
+            quantise_w(2, [2 * i, 2 * i + 1])
+            add_bias(i, 0)
+
+        turn_w(3)
+        turn_x(2)
+        empty_w(3, every_pass)
+        empty_x(2)
+        quantise_w(3, [0])
+        apply_gain(0, 0)
+        quantise_w(3, [1, 2, 3])
+        apply_gain(1, 0)
+        quantise_x(2, 0)
+        quantise_x(2, 1)
+        widen_on_vector(3, [2, 3])
+        for q in (2, 3):
+            readout_quarter(0, q)
+            readout_quarter(1, q)
+        widen_on_scalar(SCALAR_TILES[0], 0)
+        widen_on_scalar(SCALAR_TILES[0], 1)
+        add_bias(0, 1)
+        add_bias(1, 1)
+        apply_gain(0, 1)
+        apply_gain(1, 1)
+
+        readout_half(2, 0)
+        add_bias(2, 0)
+        turn_x(3)
+        turn_z(0)
+        empty_x(3)
+        empty_z(0)
+        widen_on_scalar(SCALAR_TILES[1], 0)
+        quantise_x(3, 0)
+        apply_gain(2, 0)
+        quantise_x(3, 1)
+        quantise_z(0)
+        readout_half(2, 1)
+        add_bias(2, 1)
+        apply_gain(2, 1)
 
         for j in range(TILES):
-            last = j == TILES - 1
-            if j + 4 < TILES:
-                prepare_x(j + 4, 3)
+            to_read, to_turn, to_widen = j + LEAD, j + LEAD + 1, j + LEAD + 3
+            if to_turn < TILES:
+                turn_x(to_turn)
             if j + 1 < TILES:
-                prepare_z(j + 1)
-            if j + 5 < TILES:
-                widen(j + 5, every)
-            for h in range(2):
-                for c in (2 * h, 2 * h + 1):
-                    feedback(j, c)
-                    add_drive(j, c)
-                    if last:
-                        finish(j, 512 * c, 512 * (c + 1))
-                if not last:
-                    finish(j, 1024 * h, 1024 * (h + 1))
-                if j + 3 < TILES:
-                    readout(j + 3, h, 6 + h, 0, 512)
-                    close_half(j + 3, h)
+                turn_z(j + 1)
+            if to_turn < TILES:
+                empty_x(to_turn)
+            if j + 1 < TILES:
+                empty_z(j + 1)
+            if j > 0:
+                finish_half(j - 1, 1)
+            else:
+                widen_on_scalar(SCALAR_TILES[1], 1)
+
+            for c in (0, 1):
+                feedback(j, c)
+                add_drive(j, c)
+            finish_half(j, 0)
+            if to_turn < TILES:
+                quantise_x(to_turn, 0)
+                quantise_x(to_turn, 1)
+            if to_read < TILES:
+                readout_half(to_read, 0)
+                add_bias(to_read, 0)
+            if j + 1 < TILES:
+                quantise_z(j + 1)
+
+            feedback(j, 2)
+            add_drive(j, 2)
+            if to_read < TILES:
+                apply_gain(to_read, 0)
+            feedback(j, CHUNKS - 1)
+            add_drive(j, CHUNKS - 1)
+            if to_widen < TILES:
+                widen_on_vector(to_widen, [0, 1])
+            if to_read < TILES:
+                readout_half(to_read, 1)
+                add_bias(to_read, 1)
+            if to_widen < TILES:
+                widen_on_vector(to_widen, [2])
+            if to_read < TILES:
+                apply_gain(to_read, 1)
+            if to_widen < TILES:
+                widen_on_vector(to_widen, [3])
+        finish_half(TILES - 1, 1)

@@ -27,7 +27,7 @@ PASSES_2 = N // PASS
 SCALE_RUN = 128
 QUARTER = 256
 CHUNKS = K // BANK
-SCALAR_TILES = (4, 5)
+SCALAR_TILES = (4, 5, 7)
 LEAD = 3
 
 
@@ -52,6 +52,7 @@ def tile_reservoir_readout_feedback_d4_kernel(
 
         ident = keep.tile([P, P], F32, name="ident")
         table_probe = keep.tile([P, 1], F32, name="table_probe")
+        zeros = keep.tile([P, BANK], BF16, name="zeros")
         bias_pairs = keep.tile([P, 4], F32, name="bias_pairs")
         gain_pairs = keep.tile([P, 4], F32, name="gain_pairs")
         bias = keep.tile([P, N], BF16, name="bias")
@@ -66,9 +67,9 @@ def tile_reservoir_readout_feedback_d4_kernel(
         w_raw = [work.tile([P, K], BF16, name="w_raw%d" % r, tag="rows", bufs=W_TILES) for r in range(W_TILES)]
 
         make_identity(nc, ident[:])
-        nc.gpsimd.memset(fb_scales[:].rearrange("p g n -> p (g n)").bitcast(I32), 0)
-        nc.vector.memset(table_probe[:], 0.0)
-        nc.scalar.activation(out=table_probe[:], in_=table_probe[:], func=ACT.Tanh)
+        nc.vector.memset(zeros[:].bitcast(I32), 0)
+        nc.scalar.activation(out=table_probe[:], in_=zeros[:, 0:1], func=ACT.Tanh)
+        nc.vector.memset(fb_scales[:].rearrange("p g n -> p (g n)").bitcast(I32), 0)
 
         def load_x(i):
             nc.sync.dma_start(out=x8[i][:], in_=x_bytes[rows(i), :])
@@ -116,6 +117,11 @@ def tile_reservoir_readout_feedback_d4_kernel(
             for slot, src in enumerate(sources):
                 nc.tensor.transpose(turned[:, slot, :], src, ident[:])
             return turned
+
+        def keep_clock_up(count, width):
+            unread = bank([P, BANK], "unread")
+            for n in range(count):
+                nc.tensor.matmul(unread[:, 0:width], zeros[:, 0:P], zeros[:, 0:width], start=True, stop=True)
 
         def interleave(dst, turned):
             nc.scalar.copy(
@@ -204,8 +210,8 @@ def tile_reservoir_readout_feedback_d4_kernel(
                 return w_split[r][:].bitcast(F32)[:, part(2 * g + u, P)]
             return w_raw[r][:].bitcast(F32)[:, 2 * P * g + u : 2 * P * (g + 1) : 2]
 
-        def turn_w(q):
-            for g in range(PASSES_1):
+        def turn_w(q, passes):
+            for g in passes:
                 w_turned[q, g] = turn([w_pairs(2 * q + a, g, u) for a in range(2) for u in range(2)], "wT%d_%d" % (q, g))
 
         def empty_w(q, passes):
@@ -307,16 +313,22 @@ def tile_reservoir_readout_feedback_d4_kernel(
                 finish(i, part(2 * h + 1, BANK))
 
         every_pass = range(PASSES_1)
+        keep_clock_up(4, BANK)
         spread_bias_and_gain()
+        keep_clock_up(2, BANK)
         widen_on_vector(0, every_pass)
         turn_x(0)
+        keep_clock_up(1, QUARTER)
         empty_x(0)
         quantise_x(0, 0)
         widen_on_vector(1, [0])
         quantise_x(0, 1)
         widen_on_vector(1, [1, 2, 3])
 
-        turn_w(0)
+        turn_w(0, [0, 1])
+        keep_clock_up(1, QUARTER)
+        turn_w(0, [2, 3])
+        keep_clock_up(1, QUARTER)
         empty_w(0, every_pass)
         quantise_w(0, every_pass)
         turn_x(1)
@@ -325,7 +337,9 @@ def tile_reservoir_readout_feedback_d4_kernel(
         split_w(4, nc.vector.tensor_copy)
         quantise_x(1, 1)
 
-        turn_w(1)
+        turn_w(1, [0, 1])
+        keep_clock_up(1, QUARTER)
+        turn_w(1, [2, 3])
         empty_w(1, [0, 1])
         split_w(5, nc.scalar.copy)
         empty_w(1, [2, 3])
@@ -339,7 +353,7 @@ def tile_reservoir_readout_feedback_d4_kernel(
         readout_quarter(0, 0)
         readout_quarter(1, 0)
 
-        turn_w(2)
+        turn_w(2, every_pass)
         empty_w(2, every_pass)
         readout_quarter(0, 1)
         readout_quarter(1, 1)
@@ -347,7 +361,7 @@ def tile_reservoir_readout_feedback_d4_kernel(
             quantise_w(2, [2 * i, 2 * i + 1])
             add_bias(i, 0)
 
-        turn_w(3)
+        turn_w(3, every_pass)
         turn_x(2)
         empty_w(3, every_pass)
         empty_x(2)
@@ -361,8 +375,8 @@ def tile_reservoir_readout_feedback_d4_kernel(
         for q in (2, 3):
             readout_quarter(0, q)
             readout_quarter(1, q)
-        widen_on_scalar(SCALAR_TILES[0], 0)
-        widen_on_scalar(SCALAR_TILES[0], 1)
+        widen_on_scalar(4, 0)
+        widen_on_scalar(4, 1)
         add_bias(0, 1)
         add_bias(1, 1)
         apply_gain(0, 1)
@@ -374,7 +388,7 @@ def tile_reservoir_readout_feedback_d4_kernel(
         turn_z(0)
         empty_x(3)
         empty_z(0)
-        widen_on_scalar(SCALAR_TILES[1], 0)
+        widen_on_scalar(5, 0)
         quantise_x(3, 0)
         apply_gain(2, 0)
         quantise_x(3, 1)
@@ -385,6 +399,7 @@ def tile_reservoir_readout_feedback_d4_kernel(
 
         for j in range(TILES):
             to_read, to_turn, to_widen = j + LEAD, j + LEAD + 1, j + LEAD + 3
+            vector_widens = to_widen < TILES and to_widen not in SCALAR_TILES
             if to_turn < TILES:
                 turn_x(to_turn)
             if j + 1 < TILES:
@@ -395,13 +410,15 @@ def tile_reservoir_readout_feedback_d4_kernel(
                 empty_z(j + 1)
             if j > 0:
                 finish_half(j - 1, 1)
-            else:
-                widen_on_scalar(SCALAR_TILES[1], 1)
+            if to_turn + 1 in SCALAR_TILES:
+                widen_on_scalar(to_turn + 1, 1)
 
             for c in (0, 1):
                 feedback(j, c)
                 add_drive(j, c)
             finish_half(j, 0)
+            if to_widen in SCALAR_TILES:
+                widen_on_scalar(to_widen, 0)
             if to_turn < TILES:
                 quantise_x(to_turn, 0)
                 quantise_x(to_turn, 1)
@@ -417,15 +434,15 @@ def tile_reservoir_readout_feedback_d4_kernel(
                 apply_gain(to_read, 0)
             feedback(j, CHUNKS - 1)
             add_drive(j, CHUNKS - 1)
-            if to_widen < TILES:
+            if vector_widens:
                 widen_on_vector(to_widen, [0, 1])
             if to_read < TILES:
                 readout_half(to_read, 1)
                 add_bias(to_read, 1)
-            if to_widen < TILES:
+            if vector_widens:
                 widen_on_vector(to_widen, [2])
             if to_read < TILES:
                 apply_gain(to_read, 1)
-            if to_widen < TILES:
+            if vector_widens:
                 widen_on_vector(to_widen, [3])
         finish_half(TILES - 1, 1)

from contextlib import ExitStack

import concourse.mybir as mybir
from concourse.masks import make_identity

T, K, N = 1024, 2048, 1024
FLOPS = 2 * (2 * T * K * N)

F32 = mybir.dt.float32
BF16 = mybir.dt.bfloat16
I32 = mybir.dt.int32
U32 = mybir.dt.uint32
U8 = mybir.dt.uint8
FP8 = mybir.dt.float8_e4m3fn
FP8X4 = mybir.dt.float8_e4m3fn_x4
FP4X4 = mybir.dt.float4_e2m1fn_x4
ALU = mybir.AluOpType
ACT = mybir.ActivationFunctionType

P = 128
PASS = 512
BANK = 512
TILES = T // P
W_TILES = N // P
PASSES_1 = K // PASS
PASSES_2 = N // PASS
SCALE_RUN = 128
QUARTER = 256
CHUNKS = K // BANK
SCALAR_TILES = (4, 5, 7)
LEAD = 3


def tile_reservoir_readout_feedback_d4_kernel(
    tc, x_bytes, x_scale, w_out, b_out, fb_gain, w_fb_words, w_fb_scales, drive, out_0, out_1
):
    nc = tc.nc
    with ExitStack() as ctx:
        keep = ctx.enter_context(tc.tile_pool(name="keep", bufs=1))
        work = ctx.enter_context(tc.tile_pool(name="work", bufs=2))
        psum = ctx.enter_context(tc.psum_pool(name="psum", bufs=8))
        ctx.enter_context(tc.manual_schedule())

        def bank(shape, name):
            return psum.tile(shape, F32, name=name, tag="bank")

        def rows(i):
            return slice(i * P, (i + 1) * P)

        def part(n, width):
            return slice(n * width, (n + 1) * width)

        ident = keep.tile([P, P], F32, name="ident")
        table_probe = keep.tile([P, 1], F32, name="table_probe")
        zeros = keep.tile([P, BANK], BF16, name="zeros")
        bias_pairs = keep.tile([P, 4], F32, name="bias_pairs")
        gain_pairs = keep.tile([P, 4], F32, name="gain_pairs")
        bias = keep.tile([P, N], BF16, name="bias")
        gain = keep.tile([P, N], BF16, name="gain")
        xs = keep.tile([P, TILES, K // SCALE_RUN], F32, name="xs")
        w_codes = keep.tile([P, PASSES_1, N], U32, name="w_codes", align_bytes=64)
        w_scales = keep.tile([P, PASSES_1, N], U8, name="w_scales", align_bytes=64)
        fb_words = keep.tile([P, PASSES_2, 2 * K], U8, name="fb_words", align_bytes=64)
        fb_scales = keep.tile([P, PASSES_2, K], U8, name="fb_scales", align_bytes=64)
        x8 = [keep.tile([P, K], U8, name="xbytes%d" % i) for i in range(TILES)]
        drv = [keep.tile([P, K], BF16, name="drive%d" % i) for i in range(TILES)]
        w_raw = [work.tile([P, K], BF16, name="w_raw%d" % r, tag="rows", bufs=W_TILES) for r in range(W_TILES)]

        make_identity(nc, ident[:])
        nc.vector.memset(zeros[:].bitcast(I32), 0)
        nc.scalar.activation(out=table_probe[:], in_=zeros[:, 0:1], func=ACT.Tanh)
        nc.vector.memset(fb_scales[:].rearrange("p g n -> p (g n)").bitcast(I32), 0)

        def load_x(i):
            nc.sync.dma_start(out=x8[i][:], in_=x_bytes[rows(i), :])

        def load_w(r, cols=slice(0, K)):
            nc.sync.dma_start(out=w_raw[r][:, cols], in_=w_out[rows(r), cols])

        scale_rows = x_scale.rearrange("(i p) j -> p i j", p=P)
        nc.sync.dma_start(out=bias_pairs[:].bitcast(BF16), in_=b_out.rearrange("(p j) -> p j", p=P))
        nc.sync.dma_start(out=gain_pairs[:].bitcast(BF16), in_=fb_gain.rearrange("(p j) -> p j", p=P))
        nc.sync.dma_start(out=xs[:, 0, :], in_=scale_rows[:, 0, :])
        load_x(0)
        for half in range(2):
            load_w(0, part(half, K // 2))
            load_w(1, part(half, K // 2))
        nc.sync.dma_start(out=xs[:, 1:, :], in_=scale_rows[:, 1:, :])
        load_x(1)
        for r in range(2, 6):
            load_w(r)
        load_x(2)
        load_w(6)
        load_w(7)
        load_x(3)
        load_x(4)
        for quadrant in range(4):
            nc.sync.dma_start(
                out=fb_scales[32 * quadrant : 32 * quadrant + 4, :, :].bitcast(I32),
                in_=w_fb_scales[:, part(quadrant, 4), :].rearrange("g r n -> r g n").bitcast(I32),
            )
        for g in range(PASSES_2):
            nc.sync.dma_start(out=fb_words[:, g, :].bitcast(I32), in_=w_fb_words[g].bitcast(I32))
        for i in range(TILES):
            nc.sync.dma_start(out=drv[i][:], in_=drive[rows(i), :])
            if i + 5 < TILES:
                load_x(i + 5)

        def to_split_order(copy, dst, src):
            copy(
                out=dst.bitcast(F32).rearrange("t (g u p) -> t g u p", u=2, p=P),
                in_=src.bitcast(F32).rearrange("t (g p u) -> t g u p", u=2, p=P),
            )

        def turn(sources, name):
            turned = bank([P, 4, P], name)
            for slot, src in enumerate(sources):
                nc.tensor.transpose(turned[:, slot, :], src, ident[:])
            return turned

        def keep_clock_up(count, width):
            unread = bank([P, BANK], "unread")
            for n in range(count):
                nc.tensor.matmul(unread[:, 0:width], zeros[:, 0:P], zeros[:, 0:width], start=True, stop=True)

        def interleave(dst, turned):
            nc.scalar.copy(
                out=dst.bitcast(F32).rearrange("p (a r u) -> p a r u", a=2, u=2),
                in_=turned[:].rearrange("p (a u) r -> p a r u", u=2),
            )

        def spread(pairs, name):
            return turn([pairs[:, j : j + 1].to_broadcast([P, P]) for j in range(4)], name)

        def spread_bias_and_gain():
            nc.scalar.copy(
                out=bias[:].bitcast(F32).rearrange("t (p j) -> t p j", j=4),
                in_=spread(bias_pairs, "bias_spread")[:].rearrange("t j p -> t p j"),
            )
            spread_gain = spread(gain_pairs, "gain_spread")
            for h in range(PASSES_2):
                nc.scalar.copy(
                    out=gain[:, part(h, PASS)].bitcast(F32).rearrange("t (u c a) -> t u c a", u=2, a=2),
                    in_=spread_gain[:, :, part(h, P // 2)].rearrange("t (a u) c -> t u c a", u=2),
                )

        x_split, x_plain, x_turned, x_grouped, x_codes, x_scales = {}, {}, {}, {}, {}, {}

        def split_tile(name):
            return work.tile([P, K], BF16, name=name, tag="split", bufs=6)

        def scaled_run(i, j):
            return x8[i][:, part(j, SCALE_RUN)].bitcast(FP8), xs[:, i, j : j + 1]

        def widen_on_vector(i, passes):
            if i not in x_split:
                x_split[i] = split_tile("x_split%d" % i)
            by_pair = x_split[i][:].rearrange("t (g u p e) -> t g p u e", g=PASSES_1, u=2, e=2)
            for g in passes:
                for q in range(4):
                    codes, scale = scaled_run(i, 4 * g + q)
                    nc.vector.tensor_scalar(
                        out=by_pair[:, g, part(q, 32)],
                        in0=codes.rearrange("t (p u e) -> t p u e", u=2, e=2),
                        scalar1=scale,
                        scalar2=None,
                        op0=ALU.mult,
                    )

        def widen_on_scalar(i, half):
            if half == 0:
                x_split[i] = split_tile("x_split%d" % i)
                x_plain[i] = work.tile([P, K], BF16, name="x_plain%d" % i, tag="x_plain")
            for j in range(8 * half, 8 * half + 8):
                codes, scale = scaled_run(i, j)
                nc.scalar.activation(out=x_plain[i][:, part(j, SCALE_RUN)], in_=codes, func=ACT.Copy, scale=scale)
            cols = part(half, K // 2)
            to_split_order(nc.scalar.copy, x_split[i][:, cols], x_plain[i][:, cols])

        def turn_x(i):
            pairs = x_split[i][:].bitcast(F32)
            for half in range(2):
                x_turned[i, half] = turn([pairs[:, part(4 * half + s, P)] for s in range(4)], "xT%d_%d" % (i, half))

        def empty_x(i):
            x_grouped[i] = work.tile([P, K], BF16, name="x_grouped%d" % i, tag="x_grouped", align_bytes=64)
            for half in range(2):
                interleave(x_grouped[i][:, part(half, K // 2)], x_turned[i, half])

        def quantise_x(i, half):
            if half == 0:
                x_codes[i] = work.tile([P, PASSES_1 * P], U32, name="x_codes%d" % i, tag="x_codes", bufs=5, align_bytes=64)
                x_scales[i] = work.tile([P, PASSES_1 * P], U8, name="x_scales%d" % i, tag="x_scales", bufs=5, align_bytes=64)
            cols = part(half, 2 * P)
            nc.vector.quantize_mx(
                out=x_codes[i][:, cols].bitcast(FP8X4), scales=x_scales[i][:, cols], in_=x_grouped[i][:, part(half, K // 2)]
            )

        w_split, w_turned, w_grouped = {}, {}, {}

        def grouped_tile(name):
            return work.tile([P, 4 * QUARTER], BF16, name=name, tag="grouped", bufs=6, align_bytes=64)

        def split_w(r, copy):
            w_split[r] = split_tile("w_split%d" % r)
            to_split_order(copy, w_split[r][:], w_raw[r][:])

        def w_pairs(r, g, u):
            if r in w_split:
                return w_split[r][:].bitcast(F32)[:, part(2 * g + u, P)]
            return w_raw[r][:].bitcast(F32)[:, 2 * P * g + u : 2 * P * (g + 1) : 2]

        def turn_w(q, passes):
            for g in passes:
                w_turned[q, g] = turn([w_pairs(2 * q + a, g, u) for a in range(2) for u in range(2)], "wT%d_%d" % (q, g))

        def empty_w(q, passes):
            for g in passes:
                w_grouped[q, g] = grouped_tile("w_grouped%d_%d" % (q, g))
                interleave(w_grouped[q, g][:], w_turned[q, g])

        def quantise_w(q, passes):
            for g in passes:
                cols = part(q, QUARTER)
                nc.vector.quantize_mx(out=w_codes[:, g, cols].bitcast(FP8X4), scales=w_scales[:, g, cols], in_=w_grouped[q, g][:])

        y_sum, y_sb, z_split, z_turned, z_grouped, z_codes, z_scales = {}, {}, {}, {}, {}, {}, {}

        def readout(i, first, width):
            h, offset = divmod(first, BANK)
            if offset == 0:
                y_sum[i, h] = bank([P, BANK], "y_sum%d_%d" % (i, h))
            cols = slice(first, first + width)
            for g in range(PASSES_1):
                nc.tensor.matmul_mx(
                    out=y_sum[i, h][:, offset : offset + width],
                    lhsT=x_codes[i][:, part(g, P)].bitcast(FP8X4),
                    lhsT_scale=x_scales[i][:, part(g, P)],
                    rhs=w_codes[:, g, cols].bitcast(FP8X4),
                    rhs_scale=w_scales[:, g, cols],
                    start=(g == 0),
                    stop=(g == PASSES_1 - 1),
                )

        def readout_quarter(i, q):
            readout(i, q * QUARTER, QUARTER)

        def readout_half(i, h):
            readout(i, h * BANK, BANK)

        def add_bias(i, h):
            if h == 0:
                y_sb[i] = work.tile([P, N], F32, name="y%d" % i, tag="rows", bufs=W_TILES)
            cols = part(h, BANK)
            nc.vector.tensor_tensor(out=y_sb[i][:, cols], in0=y_sum[i, h][:], in1=bias[:, cols], op=ALU.add)
            if h == 1:
                nc.sync.dma_start(out=out_0[rows(i), :], in_=y_sb[i][:])

        def apply_gain(i, h):
            if h == 0:
                z_split[i] = work.tile([P, N], BF16, name="z_split%d" % i, tag="z_split", bufs=4)
            cols = part(h, PASS)
            nc.vector.tensor_tensor(
                out=z_split[i][:, cols].rearrange("t (u p e) -> t u p e", u=2, e=2),
                in0=y_sb[i][:, cols].rearrange("t (p u e) -> t u p e", u=2, e=2),
                in1=gain[:, cols].rearrange("t (u p e) -> t u p e", u=2, e=2),
                op=ALU.mult,
            )

        def turn_z(i):
            pairs = z_split[i][:].bitcast(F32)
            z_turned[i] = turn([pairs[:, part(s, P)] for s in range(4)], "zT%d" % i)

        def empty_z(i):
            z_grouped[i] = grouped_tile("z_grouped%d" % i)
            interleave(z_grouped[i][:], z_turned[i])

        def quantise_z(i):
            z_codes[i] = work.tile([P, PASSES_2 * P], U32, name="z_codes%d" % i, tag="z_codes", bufs=3, align_bytes=64)
            z_scales[i] = work.tile([P, PASSES_2 * P], U8, name="z_scales%d" % i, tag="z_scales", bufs=3, align_bytes=64)
            nc.vector.quantize_mx(out=z_codes[i][:].bitcast(FP8X4), scales=z_scales[i][:], in_=z_grouped[i][:])

        f_sum, state = {}, {}

        def feedback(i, c):
            f_sum[i, c] = bank([P, BANK], "f_sum%d_%d" % (i, c))
            for g in range(PASSES_2):
                nc.tensor.matmul_mx(
                    out=f_sum[i, c][:],
                    lhsT=z_codes[i][:, part(g, P)].bitcast(FP8X4),
                    lhsT_scale=z_scales[i][:, part(g, P)],
                    rhs=fb_words[:, g, part(c, 2 * BANK)].bitcast(FP4X4),
                    rhs_scale=fb_scales[:, g, part(c, BANK)],
                    start=(g == 0),
                    stop=(g == PASSES_2 - 1),
                )

        def add_drive(i, c):
            if c == 0:
                state[i] = work.tile([P, K], F32, name="state%d" % i, tag="state", bufs=3)
            cols = part(c, BANK)
            nc.vector.tensor_tensor(out=state[i][:, cols], in0=f_sum[i, c][:], in1=drv[i][:, cols], op=ALU.add)

        def finish(i, cols):
            nc.scalar.activation(out=state[i][:, cols], in_=state[i][:, cols], func=ACT.Tanh)
            nc.sync.dma_start(out=out_1[rows(i), cols], in_=state[i][:, cols])

        def finish_half(i, h):
            if i + LEAD < TILES:
                finish(i, part(h, 2 * BANK))
            else:
                finish(i, part(2 * h, BANK))
                finish(i, part(2 * h + 1, BANK))

        every_pass = range(PASSES_1)
        keep_clock_up(4, BANK)
        spread_bias_and_gain()
        keep_clock_up(2, BANK)
        widen_on_vector(0, every_pass)
        turn_x(0)
        keep_clock_up(1, QUARTER)
        empty_x(0)
        quantise_x(0, 0)
        widen_on_vector(1, [0])
        quantise_x(0, 1)
        widen_on_vector(1, [1, 2, 3])

        turn_w(0, [0, 1])
        keep_clock_up(1, QUARTER)
        turn_w(0, [2, 3])
        keep_clock_up(1, QUARTER)
        empty_w(0, every_pass)
        quantise_w(0, every_pass)
        turn_x(1)
        empty_x(1)
        quantise_x(1, 0)
        split_w(4, nc.vector.tensor_copy)
        quantise_x(1, 1)

        turn_w(1, [0, 1])
        keep_clock_up(1, QUARTER)
        turn_w(1, [2, 3])
        empty_w(1, [0, 1])
        split_w(5, nc.scalar.copy)
        empty_w(1, [2, 3])
        split_w(7, nc.scalar.copy)
        quantise_w(1, [0, 1])
        widen_on_vector(2, [0, 1])
        split_w(6, nc.vector.tensor_copy)
        quantise_w(1, [2, 3])
        widen_on_vector(2, [2, 3])
        widen_on_vector(3, [0, 1])
        readout_quarter(0, 0)
        readout_quarter(1, 0)

        turn_w(2, every_pass)
        empty_w(2, every_pass)
        readout_quarter(0, 1)
        readout_quarter(1, 1)
        for i in range(2):
            quantise_w(2, [2 * i, 2 * i + 1])
            add_bias(i, 0)

        turn_w(3, every_pass)
        turn_x(2)
        empty_w(3, every_pass)
        empty_x(2)
        quantise_w(3, [0])
        apply_gain(0, 0)
        quantise_w(3, [1, 2, 3])
        apply_gain(1, 0)
        quantise_x(2, 0)
        quantise_x(2, 1)
        widen_on_vector(3, [2, 3])
        for q in (2, 3):
            readout_quarter(0, q)
            readout_quarter(1, q)
        widen_on_scalar(4, 0)
        widen_on_scalar(4, 1)
        add_bias(0, 1)
        add_bias(1, 1)
        apply_gain(0, 1)
        apply_gain(1, 1)

        readout_half(2, 0)
        add_bias(2, 0)
        turn_x(3)
        turn_z(0)
        empty_x(3)
        empty_z(0)
        widen_on_scalar(5, 0)
        quantise_x(3, 0)
        apply_gain(2, 0)
        quantise_x(3, 1)
        quantise_z(0)
        readout_half(2, 1)
        add_bias(2, 1)
        apply_gain(2, 1)

        for j in range(TILES):
            to_read, to_turn, to_widen = j + LEAD, j + LEAD + 1, j + LEAD + 3
            vector_widens = to_widen < TILES and to_widen not in SCALAR_TILES
            if to_turn < TILES:
                turn_x(to_turn)
            if j + 1 < TILES:
                turn_z(j + 1)
            if to_turn < TILES:
                empty_x(to_turn)
            if j + 1 < TILES:
                empty_z(j + 1)
            if j > 0:
                finish_half(j - 1, 1)
            if to_turn + 1 in SCALAR_TILES:
                widen_on_scalar(to_turn + 1, 1)

            for c in (0, 1):
                feedback(j, c)
                add_drive(j, c)
            finish_half(j, 0)
            if to_widen in SCALAR_TILES:
                widen_on_scalar(to_widen, 0)
            if to_turn < TILES:
                quantise_x(to_turn, 0)
                quantise_x(to_turn, 1)
            if to_read < TILES:
                readout_half(to_read, 0)
                add_bias(to_read, 0)
            if j + 1 < TILES:
                quantise_z(j + 1)

            feedback(j, 2)
            add_drive(j, 2)
            if to_read < TILES:
                apply_gain(to_read, 0)
            feedback(j, CHUNKS - 1)
            add_drive(j, CHUNKS - 1)
            if vector_widens:
                widen_on_vector(to_widen, [0, 1])
            if to_read < TILES:
                readout_half(to_read, 1)
                add_bias(to_read, 1)
            if vector_widens:
                widen_on_vector(to_widen, [2])
            if to_read < TILES:
                apply_gain(to_read, 1)
            if vector_widens:
                widen_on_vector(to_widen, [3])
        finish_half(TILES - 1, 1)
